import numpy as np, ml_dtypes
CORES = [83,85,87,115,117,119]
N = 6
C = 64
def setup_inputs(rng):
    u = np.triu(np.ones((128, 128), np.float32)).astype(ml_dtypes.bfloat16)
    return {"x": rng.standard_normal((N, 128, C), dtype=np.float32).astype(ml_dtypes.bfloat16), "u": np.broadcast_to(u, (N, 128, 128)).copy()}
def setup_inputs_big(rng):
    d = setup_inputs(rng)
    for k in ("x",): d[k] = (d[k].astype(np.float32) * 1048576.0).astype(d[k].dtype)
    return d
def setup_inputs_small(rng):
    d = setup_inputs(rng)
    for k in ("x",): d[k] = (d[k].astype(np.float32) * (1 / 1048576.0)).astype(d[k].dtype)
    return d
def setup_inputs_apart(rng):
    d = setup_inputs(rng)
    f = (10.0 ** rng.permutation(np.linspace(-1.5, 1.5, N))).astype(np.float32).reshape(N, 1, 1)
    for k in ("x",): d[k] = (d[k].astype(np.float32) * f).astype(d[k].dtype)
    return d
def reference(x, u):
    X, U = x.astype(np.float64), u.astype(np.float64)
    y = np.zeros((N, 128, C)); c = np.zeros(C)
    for r in range(N):
        y[r] = U[r].T @ X[r] + c
        c = c + X[r].sum(axis=0)
    return {"y": y.astype(ml_dtypes.bfloat16 if x.dtype != np.float64 else np.float64)}

from concourse.bass import DstId, RemoteDMATransfer

N = 6
C = 64
ENGINES = 8

SCRATCH = {
    "xs": ("sbuf", [128, C], "bfloat16"),
    "us": ("sbuf", [128, 128], "bfloat16"),
    "ones": ("sbuf", [128, 128], "bfloat16"),
    "land": ("sbuf", [128, (N - 1) * C], "bfloat16"),
    "ys": ("sbuf", [128, C], "bfloat16"),
    "acc": ("psum", [128, C], "float32"),
}
SEMAPHORES = ["xl", "ul", "on", "sent", "mm", "cp", "st"] + ["a%d" % s for s in range(N - 1)]


def rank_program(g, core, T, topo):
    r = T.rank_of(core)
    if r is None:
        return
    sem = T.sem

    def plan(s):
        src = T.cores[s]
        later = list(T.cores[s + 1:])
        dd = [d for d in later if topo.chip(d) != topo.chip(src)] + \
             [d for d in later if topo.chip(d) == topo.chip(src)]
        allowed = None
        for d in dd:
            assert topo.may_write(src, d)
            allowed = topo.mask(src, d) if allowed is None else allowed & topo.mask(src, d)
        if allowed is None:
            return [], 0, 0
        bits = [b for b in range(allowed.bit_length()) if (allowed >> b) & 1]
        n = min(ENGINES, len(bits))
        m = 0
        for b in bits[::len(bits) // n][:n]:
            m |= 1 << b
        return dd, m, n

    g.sync.dma_start(T.xs[:], T.x[:]).then_inc(sem.xl, 16)
    g.sync.dma_start(T.us[:], T.u[:]).then_inc(sem.ul, 16)
    if r > 0:
        g.vector.memset(T.ones[:], 1.0).then_inc(sem.on, 1)

    dests, mask, n_eng = plan(r)
    if dests:
        ids = []
        for d in dests:
            a = topo.addr(d)
            ids.append(DstId(rid=a[0], pnc=a[1]))
        g.wait_ge(sem.xl, 16)
        g.remote_dma_fused(
            [RemoteDMATransfer(dst_ids=ids, dma_engine_mask=mask, remote_sem=sem["a%d" % r],
                               srcs=[T.xs[:]], dsts=[T.land[:, r * C:(r + 1) * C] for d in dests], alu_op=0)],
            local_sem=sem.sent)

    g.tensor.wait_ge(sem.xl, 16)
    g.tensor.wait_ge(sem.ul, 16)
    g.tensor.matmul(T.acc[:], T.us[:], T.xs[:], True, r == 0).then_inc(sem.mm, 1)
    if r > 0:
        g.tensor.wait_ge(sem.on, 1)
    for s in range(r - 1, -1, -1):
        g.tensor.wait_ge(sem["a%d" % s], plan(s)[2])
        g.tensor.matmul(T.acc[:], T.ones[:], T.land[:, s * C:(s + 1) * C], False, s == 0).then_inc(sem.mm, 1)

    g.vector.wait_ge(sem.mm, r + 1)
    g.vector.tensor_copy(T.ys[:], T.acc[:]).then_inc(sem.cp, 1)
    g.sync.wait_ge(sem.cp, 1)
    g.sync.dma_start(T.y[:], T.ys[:]).then_inc(sem.st, 16)
    g.sync.wait_ge(sem.st, 16)
    if dests:
        g.wait_ge(sem.sent, n_eng)
